import numpy as np
import ml_dtypes


def mxq(x, axis, fmt="e4m3"):
    dtype, down = {"e4m3": (ml_dtypes.float8_e4m3fn, 7), "e5m2": (ml_dtypes.float8_e5m2, 14)}[fmt]
    v = np.moveaxis(np.asarray(x, np.float32).astype(ml_dtypes.bfloat16).astype(np.float64), axis, -1)
    blocks = v.reshape(v.shape[:-1] + (-1, 32))
    amax = np.abs(blocks).max(-1, keepdims=True)
    byte = np.maximum(np.where(amax > 0, np.frexp(amax)[1] - 1 + 127, 0) - down, 1)
    scale = np.exp2(byte - 127.0)
    codes = (blocks / scale).astype(np.float32).astype(dtype).astype(np.float64)
    return np.moveaxis((codes * scale).reshape(v.shape), -1, axis)


WIDE = False


def mx_kscale(k):
    if not WIDE:
        return np.ones(k)
    levels = np.array([10, -10, 5, -5, 0])
    if k % 512:
        return np.exp2(np.random.permutation(np.resize(levels, k // 32))).repeat(32)
    a = np.empty((k // 512, 16))
    for p in range(k // 512):
        a[p, :8] = np.random.permutation(np.resize(levels, 8))
        for g in range(8):
            far = levels[np.abs(levels - a[p, g]) >= 10]
            a[p, g + 8] = far[np.random.randint(len(far))]
    return np.exp2(a.ravel()).repeat(32)


def f64(x):
    return np.asarray(x).astype(np.float64)


def striped(idx):
    return np.tile(idx.reshape(-1, 16).T, (8, 1)).astype(np.uint16)


def unstriped(offs):
    return offs[:16].T.reshape(-1).astype(np.int64)


def striped8(idx):
    return np.concatenate([x.reshape(-1, 16).T for x in idx]).astype(np.uint16)


def runs(offs, k):
    lists = np.stack([offs[16 * r : 16 * r + 16].T.reshape(-1) for r in range(8)]).astype(np.int64)
    return lists[np.arange(k) % 512 // 64]


def pack_weight(w):
    k, n = w.shape
    w = f64(np.asarray(w, np.float32).astype(ml_dtypes.bfloat16)).reshape(k // 32, 32, n)
    amax = np.abs(w).max(1)
    byte = np.clip(np.where(amax > 0, np.frexp(amax)[1] - 1 + 127 - 7, 1), 1, 254)
    scaled = (w * np.exp2(127.0 - byte)[:, None, :]).reshape(k, n).astype(np.float32)
    words = np.ascontiguousarray(scaled.reshape(k // 512, 128, 4, n).transpose(0, 1, 3, 2)).astype(ml_dtypes.float8_e4m3fn).view(np.uint8)
    return words, np.ascontiguousarray(byte.astype(np.uint8).reshape(k // 512, 16, n))


def unpack_weight(words, scales):
    g, p, n, _ = words.shape
    vals = np.ascontiguousarray(words).view(ml_dtypes.float8_e4m3fn).astype(np.float64) * np.repeat(np.exp2(scales.astype(np.float64) - 127.0), 8, axis=1)[..., None]
    return vals.transpose(0, 1, 3, 2).reshape(g * 512, n)


def sigmoid(v):
    return 1.0 / (1.0 + np.exp(-np.maximum(v, -700.0)))


K, T, S, H, C = 512, 2048, 512, 512, 512


def setup_inputs():
    n = np.random.standard_normal
    s = mx_kscale(K)[:, None]
    packed_xT = pack_weight(n((K, T)) * s)
    return {
        "x_words": packed_xT[0],
        "x_scales": packed_xT[1],
        "w1": (n((K, H)) / np.sqrt(K) / s).astype(np.float32),
        "w2": (n((K, H)) / np.sqrt(K) / s).astype(np.float32),
        "gs": (np.random.uniform(0.5, 1.5, (K, 1)) / s).astype(np.float32),
        "offs": striped(np.random.permutation(T)[:S]),
        "two": striped(np.random.permutation(T)[:S]),
        "n1": striped8(np.stack([np.random.permutation(S) for _ in range(8)])),
        "n2": striped8(np.stack([np.random.permutation(S) for _ in range(8)])),
        "cand": striped(np.random.permutation(T)[:C]),
        "n3": striped8(np.stack([np.random.permutation(S) for _ in range(8)])),
        "n4": striped8(np.stack([np.random.permutation(S) for _ in range(8)])),
    }


def reference(x_words, x_scales, w1, w2, gs, offs, two, n1, n2, cand, n3, n4):
    x_cand = unpack_weight(x_words, x_scales)[:, unstriped(cand)]
    xq = unpack_weight(x_words, x_scales)[:, unstriped(offs)]
    y = mxq(f64(w1), 0, "e4m3").T @ xq
    x_two = unpack_weight(x_words, x_scales)[:, unstriped(two)]
    d = mxq(f64(w2), 0, "e4m3").T @ x_two
    z = f64(gs) * (y * (sigmoid(d[np.arange(H)[:, None], runs(n2, H)])) - (0.5 * (y[np.arange(H)[:, None], runs(n1, H)])))
    s = 0.0625 * ((x_cand.T @ mxq(z, 0, "e4m3")))
    ex = np.exp(s)
    return np.log(ex + ex[np.arange(C)[:, None], runs(n3, C)]) - (s[np.arange(C)[:, None], runs(n4, C)])

@@ -1,0 +1,184 @@
+from contextlib import ExitStack
+
+import concourse.mybir as mybir
+
+K, T, S, H, C = 512, 2048, 512, 512, 512
+FLOPS = 2 * K * S * (H + H + C)
+
+F32 = mybir.dt.float32
+BF16 = mybir.dt.bfloat16
+I32 = mybir.dt.int32
+U32 = mybir.dt.uint32
+U16 = mybir.dt.uint16
+U8 = mybir.dt.uint8
+FP8X4 = mybir.dt.float8_e4m3fn_x4
+ACT = mybir.ActivationFunctionType
+ALU = mybir.AluOpType
+
+P = 128
+PACK = 4
+WINDOW = 2 * S
+
+
+def tile_picked_twcgateblse_none_p_kernel(
+    tc, x_words, x_scales, w1, w2, gs, offs, two, n1, n2, cand, n3, n4, out
+):
+    nc = tc.nc
+    with ExitStack() as ctx:
+        keep = ctx.enter_context(tc.tile_pool(name="keep", bufs=1))
+        psum = ctx.enter_context(tc.psum_pool(name="psum", bufs=1))
+
+        def sb(name, shape, dtype, tag=None):
+            return keep.tile(shape, dtype, name=name, tag=tag or name, align_bytes=64)
+
+        lists = {}
+
+        def load_list(name, src):
+            lists[name] = keep.tile([P, S // 16], U16, name="list_" + name)
+            nc.sync.dma_start(lists[name][:], src)
+
+        table_bytes = sb("table_bytes", [P, T], U8)
+        nc.gpsimd.memset(table_bytes[:].bitcast(I32), 0)
+        for q in range(4):
+            nc.scalar.dma_start(
+                table_bytes[32 * q : 32 * q + 4, :].bitcast(I32), x_scales[0, 4 * q : 4 * q + 4, :].bitcast(I32)
+            )
+        load_list("two", two)
+        load_list("offs", offs)
+        w2_raw = sb("w2_raw", [P, PACK, H], F32)
+        nc.sync.dma_start(w2_raw[:], w2.rearrange("(p j) c -> p j c", j=PACK))
+        table_words = sb("table_words", [P, T], I32)
+        nc.sync.dma_start(table_words[:], x_words[0].rearrange("p n t -> p (n t)").bitcast(I32))
+        load_list("cand", cand)
+        w1_raw = sb("w1_raw", [P, PACK, H], F32)
+        nc.sync.dma_start(w1_raw[:], w1.rearrange("(p j) c -> p j c", j=PACK))
+        gain = sb("gain", [P, PACK], F32)
+        nc.sync.dma_start(gain[:], gs.rearrange("(p t) o -> p (t o)", t=PACK))
+        load_list("n2", n2)
+        load_list("n1", n1)
+        load_list("n3", n3)
+        load_list("n4", n4)
+
+        warm = sb("warm", [P, 2], F32)
+        nc.vector.memset(warm[:], 0.0)
+        warm_out = sb("warm_out", [P, 2], F32)
+        nc.scalar.activation(warm_out[:, 0:1], warm[:, 0:1], ACT.Sigmoid)
+
+        win_a = [sb("win_a%d" % t, [P, WINDOW], F32) for t in range(PACK)]
+        win_b = [sb("win_b%d" % t, [P, WINDOW], F32) for t in range(PACK)]
+        for t in range(PACK):
+            nc.vector.memset(win_a[t][:, S:], 0.0)
+            nc.gpsimd.memset(win_b[t][:, S:], 0.0)
+
+        def gather_bytes(name):
+            picked = sb("bytes_" + name, [P, S], U8)
+            nc.vector.tensor_copy(picked[:], table_bytes[:].indirect(lists[name][:]))
+            return picked
+
+        def gather_words(name, tag=None):
+            picked = sb("words_" + name, [P, S], U32, tag)
+            nc.vector.tensor_copy(picked[:], table_words[:].bitcast(U32).indirect(lists[name][:]))
+            return picked
+
+        def cast_weight(copy, grouped, raw, m0, m1):
+            dst = grouped[:].rearrange("p (t m j) -> p m t j", t=PACK, j=PACK)
+            copy(dst[:, m0:m1], raw[:].rearrange("p j (m t) -> p m t j", t=PACK))
+
+        def quantize(name, grouped):
+            codes = sb(name + "_codes", [P, H], U32)
+            scales = sb(name + "_scales", [P, H], U8)
+            nc.vector.quantize_mx(out=codes[:].bitcast(FP8X4), scales=scales[:], in_=grouped[:])
+            return codes, scales
+
+        def product(tag, t, lhs, rhs):
+            acc = psum.tile([P, S], F32, name=tag + str(t), tag=tag + str(t))
+            cols = slice(P * t, P * (t + 1))
+            nc.tensor.matmul_mx(
+                out=acc[:],
+                lhsT=lhs[0][:, cols].bitcast(FP8X4),
+                lhsT_scale=lhs[1][:, cols],
+                rhs=rhs[0][:].bitcast(FP8X4),
+                rhs_scale=rhs[1][:],
+                start=True,
+                stop=True,
+            )
+            return acc
+
+        two_bytes = gather_bytes("two")
+        offs_bytes = gather_bytes("offs")
+        cand_bytes = gather_bytes("cand")
+        w2_bf = sb("w2_bf", [P, PACK * H], BF16)
+        cast_weight(nc.scalar.copy, w2_bf, w2_raw, 0, P)
+        dealt_bytes = sb("dealt_bytes", [P, C], U8)
+        nc.vector.tensor_copy(
+            dealt_bytes[:].rearrange("p (t a b) -> p a t b", t=PACK, b=16),
+            cand_bytes[:].rearrange("p (a b t) -> p a t b", t=PACK, b=16),
+        )
+        two_words = gather_words("two")
+        w2_q = quantize("w2", w2_bf)
+        d_acc = [product("bank_a", t, w2_q, (two_words, two_bytes)) for t in range(PACK)]
+        offs_words = gather_words("offs")
+        w1_bf = sb("w1_bf", [P, PACK * H], BF16)
+        cast_weight(nc.vector.tensor_copy, w1_bf, w1_raw, 0, P)
+        w1_q = quantize("w1", w1_bf)
+        cand_words = gather_words("cand", "w1_bf")
+        y_acc = [product("bank_b", t, w1_q, (offs_words, offs_bytes)) for t in range(PACK)]
+        dealt_words = sb("dealt_words", [P, C], U32)
+        nc.vector.tensor_copy(
+            dealt_words[:].rearrange("p (t a b) -> p a t b", t=PACK, b=4),
+            cand_words[:].rearrange("p (a b t) -> p a t b", t=PACK, b=4),
+        )
+        half_gain = sb("half_gain", [P, PACK], F32)
+        nc.vector.tensor_scalar(half_gain[:], gain[:], 0.5, None, ALU.mult)
+
+        halves = [slice(0, S // 2), slice(S // 2, S)]
+        neg_z = sb("neg_z", [P, PACK, S], F32)
+        for t in range(PACK):
+            nc.scalar.copy(win_a[t][:, :S], d_acc[t][:])
+            gate = sb("gate%d" % t, [P, S], F32)
+            nc.scalar.activation(gate[:], win_a[t][:].indirect(lists["n2"][:]), ACT.Sigmoid)
+            nc.scalar.activation(win_b[t][:, :S], y_acc[t][:], ACT.Copy, scale=half_gain[:, t : t + 1])
+            gated = sb("gated%d" % t, [P, S], F32)
+            nc.vector.scalar_tensor_tensor(gated[:], y_acc[t][:], gain[:, t : t + 1], gate[:], ALU.mult, ALU.mult)
+            for h in halves if t == PACK - 1 else [slice(0, S)]:
+                picks = lists["n1"][:, h.start // 16 : h.stop // 16]
+                nc.vector.tensor_tensor(neg_z[:, t, h], win_b[t][:].indirect(picks), gated[:, h], ALU.subtract)
+        nc.scalar.activation(warm_out[:, 1:2], win_b[PACK - 1][:, 0:1], ACT.Exp, scale=0.0)
+
+        z_bf = sb("z_bf", [P, PACK * S], BF16)
+        z_codes = sb("z_codes", [P, S], U32)
+        z_scales = sb("z_scales", [P, S], U8)
+        z_dst = z_bf[:].rearrange("p (c i t) -> p c t i", t=PACK, i=4)
+        z_src = neg_z[:].rearrange("p t (c i) -> p c t i", i=4)
+        mid = S // 8
+        nc.scalar.activation(z_dst[:, :mid], z_src[:, :mid], ACT.Copy, scale=-1.0)
+        nc.vector.tensor_scalar(z_dst[:, mid:], z_src[:, mid:], -1.0, None, ALU.mult)
+        for h in halves:
+            nc.vector.quantize_mx(
+                out=z_codes[:, h].bitcast(FP8X4), scales=z_scales[:, h], in_=z_bf[:, PACK * h.start : PACK * h.stop]
+            )
+        s_acc = [product("bank_a", t, (dealt_words, dealt_bytes), (z_codes, z_scales)) for t in range(PACK)]
+
+        sums = []
+        neg_c = []
+        ex = []
+        for t in range(PACK):
+            ex.append(sb("ex%d" % t, [P, S], F32))
+            nc.scalar.activation(ex[t][:], s_acc[t][:], ACT.Exp, scale=0.0625)
+            nc.vector.tensor_scalar(win_a[t][:, :S], s_acc[t][:], -0.0625, None, ALU.mult)
+        for t in range(PACK):
+            ex_n3 = sb("ex_n3%d" % t, [P, S], F32)
+            nc.scalar.activation(ex_n3[:], win_a[t][:].indirect(lists["n3"][:]), ACT.Exp, scale=-1.0)
+            fetched = sb("neg_c%d" % t, [P, S], F32)
+            nc.vector.tensor_copy(fetched[:], win_a[t][:].indirect(lists["n4"][:]))
+            neg_c.append(fetched)
+            total = sb("sum%d" % t, [P, S], F32)
+            nc.vector.tensor_tensor(total[:], ex[t][:], ex_n3[:], ALU.add)
+            sums.append(total)
+        out_rows = out.rearrange("(p t) j -> p t j", t=PACK)
+        for t in range(PACK):
+            logs = sb("logs%d" % t, [P, S], F32)
+            nc.scalar.activation(logs[:], sums[t][:], ACT.Ln)
+            result = sb("result%d" % t, [P, S], F32)
+            nc.vector.tensor_tensor(result[:], logs[:], neg_c[t][:], ALU.add)
+            nc.sync.dma_start(out_rows[:, t, :], result[:])

@@ -37,21 +37,20 @@ def tile_picked_twcgateblse_none_p_kernel(
             lists[name] = keep.tile([P, S // 16], U16, name="list_" + name)
             nc.sync.dma_start(lists[name][:], src)
 
-        table_bytes = sb("table_bytes", [P, T], U8)
-        nc.gpsimd.memset(table_bytes[:].bitcast(I32), 0)
+        scale_rows = sb("scale_rows", [P, T // 4], I32)
         for q in range(4):
-            nc.scalar.dma_start(
-                table_bytes[32 * q : 32 * q + 4, :].bitcast(I32), x_scales[0, 4 * q : 4 * q + 4, :].bitcast(I32)
-            )
+            nc.sync.dma_start(scale_rows[32 * q : 32 * q + 4, :], x_scales[0, 4 * q : 4 * q + 4, :].bitcast(I32))
         load_list("two", two)
-        load_list("offs", offs)
         w2_raw = sb("w2_raw", [P, PACK, H], F32)
         nc.sync.dma_start(w2_raw[:], w2.rearrange("(p j) c -> p j c", j=PACK))
+        load_list("offs", offs)
+        load_list("cand", cand)
+        w1_rows = w1.rearrange("(p j) c -> p j c", j=PACK)
+        w1_raw = [sb("w1_raw%d" % h, [P, PACK, H // 2], F32) for h in range(2)]
+        nc.sync.dma_start(w1_raw[0][:], w1_rows[:, :, : H // 2])
         table_words = sb("table_words", [P, T], I32)
         nc.sync.dma_start(table_words[:], x_words[0].rearrange("p n t -> p (n t)").bitcast(I32))
-        load_list("cand", cand)
-        w1_raw = sb("w1_raw", [P, PACK, H], F32)
-        nc.sync.dma_start(w1_raw[:], w1.rearrange("(p j) c -> p j c", j=PACK))
+        nc.sync.dma_start(w1_raw[1][:], w1_rows[:, :, H // 2 :])
         gain = sb("gain", [P, PACK], F32)
         nc.sync.dma_start(gain[:], gs.rearrange("(p t) o -> p (t o)", t=PACK))
         load_list("n2", n2)
@@ -59,16 +58,23 @@ def tile_picked_twcgateblse_none_p_kernel(
         load_list("n3", n3)
         load_list("n4", n4)
 
+        table_bytes = sb("table_bytes", [P, T], U8)
+        nc.vector.memset(table_bytes[:].bitcast(I32), 0)
         warm = sb("warm", [P, 2], F32)
-        nc.vector.memset(warm[:], 0.0)
+        nc.gpsimd.memset(warm[:], 0.0)
         warm_out = sb("warm_out", [P, 2], F32)
         nc.scalar.activation(warm_out[:, 0:1], warm[:, 0:1], ACT.Sigmoid)
 
-        win_a = [sb("win_a%d" % t, [P, WINDOW], F32) for t in range(PACK)]
         win_b = [sb("win_b%d" % t, [P, WINDOW], F32) for t in range(PACK)]
-        for t in range(PACK):
-            nc.vector.memset(win_a[t][:, S:], 0.0)
-            nc.gpsimd.memset(win_b[t][:, S:], 0.0)
+        spare = sb("spare", [P, WINDOW], F32)
+        for t in range(2):
+            nc.vector.memset(win_b[t][:, S:], 0.0)
+            nc.gpsimd.memset(win_b[t + 2][:, S:], 0.0)
+        nc.gpsimd.memset(spare[:, S:], 0.0)
+        win_a = [raw[:].rearrange("p j c -> p (j c)") for raw in (w2_raw, w1_raw[0], w1_raw[1])] + [spare[:]]
+        for q in range(4):
+            rows = slice(32 * q, 32 * q + 4)
+            nc.vector.tensor_copy(table_bytes[rows, :].bitcast(I32), scale_rows[rows, :])
 
         def gather_bytes(name):
             picked = sb("bytes_" + name, [P, S], U8)
@@ -114,12 +120,13 @@ def tile_picked_twcgateblse_none_p_kernel(
             dealt_bytes[:].rearrange("p (t a b) -> p a t b", t=PACK, b=16),
             cand_bytes[:].rearrange("p (a b t) -> p a t b", t=PACK, b=16),
         )
-        two_words = gather_words("two")
-        w2_q = quantize("w2", w2_bf)
-        d_acc = [product("bank_a", t, w2_q, (two_words, two_bytes)) for t in range(PACK)]
-        offs_words = gather_words("offs")
         w1_bf = sb("w1_bf", [P, PACK * H], BF16)
-        cast_weight(nc.vector.tensor_copy, w1_bf, w1_raw, 0, P)
+        cast_weight(nc.scalar.copy, w1_bf, w1_raw[0], 0, P // 2)
+        w2_q = quantize("w2", w2_bf)
+        two_words = gather_words("two")
+        d_acc = [product("bank_a", t, w2_q, (two_words, two_bytes)) for t in range(PACK)]
+        cast_weight(nc.vector.tensor_copy, w1_bf, w1_raw[1], P // 2, P)
+        offs_words = gather_words("offs")
         w1_q = quantize("w1", w1_bf)
         cand_words = gather_words("cand", "w1_bf")
         y_acc = [product("bank_b", t, w1_q, (offs_words, offs_bytes)) for t in range(PACK)]
@@ -129,21 +136,24 @@ def tile_picked_twcgateblse_none_p_kernel(
             cand_words[:].rearrange("p (a b t) -> p a t b", t=PACK, b=4),
         )
         half_gain = sb("half_gain", [P, PACK], F32)
-        nc.vector.tensor_scalar(half_gain[:], gain[:], 0.5, None, ALU.mult)
+        nc.gpsimd.tensor_scalar(half_gain[:], gain[:], 0.5, 0.0, ALU.mult, ALU.add)
 
         halves = [slice(0, S // 2), slice(S // 2, S)]
         neg_z = sb("neg_z", [P, PACK, S], F32)
         for t in range(PACK):
-            nc.scalar.copy(win_a[t][:, :S], d_acc[t][:])
             gate = sb("gate%d" % t, [P, S], F32)
-            nc.scalar.activation(gate[:], win_a[t][:].indirect(lists["n2"][:]), ACT.Sigmoid)
+            d_row = sb("d_row%d" % t, [P, S], F32, "gate%d" % (t - 2) if t >= 2 else None)
+            nc.scalar.copy(d_row[:], d_acc[t][:])
+            for h in halves:
+                picks = lists["n2"][:, h.start // 16 : h.stop // 16]
+                nc.scalar.activation(gate[:, h], d_row[:].indirect(picks), ACT.Sigmoid)
             nc.scalar.activation(win_b[t][:, :S], y_acc[t][:], ACT.Copy, scale=half_gain[:, t : t + 1])
             gated = sb("gated%d" % t, [P, S], F32)
             nc.vector.scalar_tensor_tensor(gated[:], y_acc[t][:], gain[:, t : t + 1], gate[:], ALU.mult, ALU.mult)
             for h in halves if t == PACK - 1 else [slice(0, S)]:
                 picks = lists["n1"][:, h.start // 16 : h.stop // 16]
                 nc.vector.tensor_tensor(neg_z[:, t, h], win_b[t][:].indirect(picks), gated[:, h], ALU.subtract)
-        nc.scalar.activation(warm_out[:, 1:2], win_b[PACK - 1][:, 0:1], ACT.Exp, scale=0.0)
+        nc.scalar.activation(warm_out[:, 1:2], gate[:, S - 1 : S], ACT.Exp)
 
         z_bf = sb("z_bf", [P, PACK * S], BF16)
         z_codes = sb("z_codes", [P, S], U32)
@@ -159,26 +169,30 @@ def tile_picked_twcgateblse_none_p_kernel(
             )
         s_acc = [product("bank_a", t, (dealt_words, dealt_bytes), (z_codes, z_scales)) for t in range(PACK)]
 
+        def exp_of_scores(dst, t):
+            nc.scalar.activation(dst, s_acc[t][:], ACT.Exp, scale=0.0625)
+
         sums = []
-        neg_c = []
-        ex = []
         for t in range(PACK):
-            ex.append(sb("ex%d" % t, [P, S], F32))
-            nc.scalar.activation(ex[t][:], s_acc[t][:], ACT.Exp, scale=0.0625)
-            nc.vector.tensor_scalar(win_a[t][:, :S], s_acc[t][:], -0.0625, None, ALU.mult)
-        for t in range(PACK):
-            ex_n3 = sb("ex_n3%d" % t, [P, S], F32)
-            nc.scalar.activation(ex_n3[:], win_a[t][:].indirect(lists["n3"][:]), ACT.Exp, scale=-1.0)
-            fetched = sb("neg_c%d" % t, [P, S], F32)
-            nc.vector.tensor_copy(fetched[:], win_a[t][:].indirect(lists["n4"][:]))
-            neg_c.append(fetched)
+            ex = sb("ex%d" % t, [P, S], F32)
+            exp_of_scores(win_b[t][:, :S], t)
+            if t < 2:
+                exp_of_scores(ex[:], t)
+            else:
+                nc.vector.tensor_copy(ex[:], win_b[t][:, :S])
+            if t == 0:
+                nc.vector.tensor_scalar(win_a[1][:, :S], s_acc[1][:], -0.0625, None, ALU.mult)
             total = sb("sum%d" % t, [P, S], F32)
-            nc.vector.tensor_tensor(total[:], ex[t][:], ex_n3[:], ALU.add)
+            nc.vector.tensor_tensor(total[:], win_b[t][:].indirect(lists["n3"][:]), ex[:], ALU.add)
             sums.append(total)
         out_rows = out.rearrange("(p t) j -> p t j", t=PACK)
-        for t in range(PACK):
+        for t in (1, 0, 2, 3):
             logs = sb("logs%d" % t, [P, S], F32)
             nc.scalar.activation(logs[:], sums[t][:], ACT.Ln)
+            if t != 1:
+                nc.scalar.activation(win_a[t][:, :S], s_acc[t][:], ACT.Copy, scale=-0.0625)
             result = sb("result%d" % t, [P, S], F32)
-            nc.vector.tensor_tensor(result[:], logs[:], neg_c[t][:], ALU.add)
-            nc.sync.dma_start(out_rows[:, t, :], result[:])
+            for h in halves if t == PACK - 1 else [slice(0, S)]:
+                picks = lists["n4"][:, h.start // 16 : h.stop // 16]
+                nc.vector.tensor_tensor(result[:, h], win_a[t].indirect(picks), logs[:, h], ALU.add)
+                nc.sync.dma_start(out_rows[:, t, h], result[:, h])

@@ -47,9 +47,9 @@ def tile_picked_twcgateblse_none_p_kernel(
         load_list("cand", cand)
         w1_rows = w1.rearrange("(p j) c -> p j c", j=PACK)
         w1_raw = [sb("w1_raw%d" % h, [P, PACK, H // 2], F32) for h in range(2)]
-        nc.sync.dma_start(w1_raw[0][:], w1_rows[:, :, : H // 2])
         table_words = sb("table_words", [P, T], I32)
         nc.sync.dma_start(table_words[:], x_words[0].rearrange("p n t -> p (n t)").bitcast(I32))
+        nc.sync.dma_start(w1_raw[0][:], w1_rows[:, :, : H // 2])
         nc.sync.dma_start(w1_raw[1][:], w1_rows[:, :, H // 2 :])
         gain = sb("gain", [P, PACK], F32)
         nc.sync.dma_start(gain[:], gs.rearrange("(p t) o -> p (t o)", t=PACK))
@@ -66,18 +66,17 @@ def tile_picked_twcgateblse_none_p_kernel(
         nc.scalar.activation(warm_out[:, 0:1], warm[:, 0:1], ACT.Sigmoid)
 
         win_b = [sb("win_b%d" % t, [P, WINDOW], F32) for t in range(PACK)]
-        spare = sb("spare", [P, WINDOW], F32)
+        spare = [sb("spare%d" % t, [P, WINDOW], F32) for t in range(2)]
         for t in range(2):
             nc.vector.memset(win_b[t][:, S:], 0.0)
             nc.gpsimd.memset(win_b[t + 2][:, S:], 0.0)
-        nc.gpsimd.memset(spare[:, S:], 0.0)
-        win_a = [raw[:].rearrange("p j c -> p (j c)") for raw in (w2_raw, w1_raw[0], w1_raw[1])] + [spare[:]]
+            nc.gpsimd.memset(spare[t][:, S:], 0.0)
         for q in range(4):
             rows = slice(32 * q, 32 * q + 4)
             nc.vector.tensor_copy(table_bytes[rows, :].bitcast(I32), scale_rows[rows, :])
 
-        def gather_bytes(name):
-            picked = sb("bytes_" + name, [P, S], U8)
+        def gather_bytes(name, tag=None):
+            picked = sb("bytes_" + name, [P, S], U8, tag)
             nc.vector.tensor_copy(picked[:], table_bytes[:].indirect(lists[name][:]))
             return picked
 
@@ -96,15 +95,15 @@ def tile_picked_twcgateblse_none_p_kernel(
             nc.vector.quantize_mx(out=codes[:].bitcast(FP8X4), scales=scales[:], in_=grouped[:])
             return codes, scales
 
-        def product(tag, t, lhs, rhs):
-            acc = psum.tile([P, S], F32, name=tag + str(t), tag=tag + str(t))
+        def product(tag, t, lhs, rhs, places=slice(0, S)):
+            acc = psum.tile([P, places.stop - places.start], F32, name=tag + str(t), tag=tag + str(t))
             cols = slice(P * t, P * (t + 1))
             nc.tensor.matmul_mx(
                 out=acc[:],
                 lhsT=lhs[0][:, cols].bitcast(FP8X4),
                 lhsT_scale=lhs[1][:, cols],
-                rhs=rhs[0][:].bitcast(FP8X4),
-                rhs_scale=rhs[1][:],
+                rhs=rhs[0][:, places].bitcast(FP8X4),
+                rhs_scale=rhs[1][:, places],
                 start=True,
                 stop=True,
             )
@@ -115,45 +114,64 @@ def tile_picked_twcgateblse_none_p_kernel(
         cand_bytes = gather_bytes("cand")
         w2_bf = sb("w2_bf", [P, PACK * H], BF16)
         cast_weight(nc.scalar.copy, w2_bf, w2_raw, 0, P)
-        dealt_bytes = sb("dealt_bytes", [P, C], U8)
-        nc.vector.tensor_copy(
-            dealt_bytes[:].rearrange("p (t a b) -> p a t b", t=PACK, b=16),
-            cand_bytes[:].rearrange("p (a b t) -> p a t b", t=PACK, b=16),
-        )
         w1_bf = sb("w1_bf", [P, PACK * H], BF16)
         cast_weight(nc.scalar.copy, w1_bf, w1_raw[0], 0, P // 2)
         w2_q = quantize("w2", w2_bf)
         two_words = gather_words("two")
         d_acc = [product("bank_a", t, w2_q, (two_words, two_bytes)) for t in range(PACK)]
+        dealt_bytes = sb("dealt_bytes", [P, C], U8, "w2_bf")
+        nc.vector.tensor_copy(
+            dealt_bytes[:].rearrange("p (t a b) -> p a t b", t=PACK, b=16),
+            cand_bytes[:].rearrange("p (a b t) -> p a t b", t=PACK, b=16),
+        )
         cast_weight(nc.vector.tensor_copy, w1_bf, w1_raw[1], P // 2, P)
         offs_words = gather_words("offs")
         w1_q = quantize("w1", w1_bf)
-        cand_words = gather_words("cand", "w1_bf")
-        y_acc = [product("bank_b", t, w1_q, (offs_words, offs_bytes)) for t in range(PACK)]
+        cand_words = gather_words("cand", "w1_raw1")
         dealt_words = sb("dealt_words", [P, C], U32)
         nc.vector.tensor_copy(
             dealt_words[:].rearrange("p (t a b) -> p a t b", t=PACK, b=4),
             cand_words[:].rearrange("p (a b t) -> p a t b", t=PACK, b=4),
         )
+        y_acc = [product("bank_b", t, w1_q, (offs_words, offs_bytes)) for t in range(PACK)]
         half_gain = sb("half_gain", [P, PACK], F32)
         nc.gpsimd.tensor_scalar(half_gain[:], gain[:], 0.5, 0.0, ALU.mult, ALU.add)
 
         halves = [slice(0, S // 2), slice(S // 2, S)]
         neg_z = sb("neg_z", [P, PACK, S], F32)
+        win_a = [raw[:].rearrange("p j c -> p (j c)") for raw in (w2_raw, neg_z)] + [spare[0][:], spare[1][:]]
+        last = PACK - 1
+        d_slots = ["w1_raw0", "w1_bf", "gate0", "gate1"]
+        d_rows = []
+
+        def empty_d(t):
+            d_rows.append(sb("d_row%d" % t, [P, S], F32, d_slots[t]))
+            nc.scalar.activation(d_rows[t][:], d_acc[t][:], ACT.Sigmoid if t == last else ACT.Copy)
+
+        empty_d(0)
         for t in range(PACK):
-            gate = sb("gate%d" % t, [P, S], F32)
-            d_row = sb("d_row%d" % t, [P, S], F32, "gate%d" % (t - 2) if t >= 2 else None)
-            nc.scalar.copy(d_row[:], d_acc[t][:])
-            for h in halves:
-                picks = lists["n2"][:, h.start // 16 : h.stop // 16]
-                nc.scalar.activation(gate[:, h], d_row[:].indirect(picks), ACT.Sigmoid)
-            nc.scalar.activation(win_b[t][:, :S], y_acc[t][:], ACT.Copy, scale=half_gain[:, t : t + 1])
             gated = sb("gated%d" % t, [P, S], F32)
-            nc.vector.scalar_tensor_tensor(gated[:], y_acc[t][:], gain[:, t : t + 1], gate[:], ALU.mult, ALU.mult)
-            for h in halves if t == PACK - 1 else [slice(0, S)]:
+            if t < last:
+                gate = sb("gate%d" % t, [P, S], F32)
+                for h in halves:
+                    picks = lists["n2"][:, h.start // 16 : h.stop // 16]
+                    nc.scalar.activation(gate[:, h], d_rows[t][:].indirect(picks), ACT.Sigmoid)
+                if t + 1 < last:
+                    empty_d(t + 1)
+                nc.scalar.activation(win_b[t][:, :S], y_acc[t][:], ACT.Copy, scale=half_gain[:, t : t + 1])
+                nc.vector.scalar_tensor_tensor(gated[:], y_acc[t][:], gain[:, t : t + 1], gate[:], ALU.mult, ALU.mult)
+            else:
+                empty_d(t)
+                y_row = sb("y_row", [P, S], F32, "gate0")
+                nc.scalar.activation(y_row[:], y_acc[t][:], ACT.Copy, scale=gain[:, t : t + 1])
+                nc.scalar.activation(win_b[t][:, :S], y_acc[t][:], ACT.Copy, scale=half_gain[:, t : t + 1])
+                for h in halves:
+                    picks = lists["n2"][:, h.start // 16 : h.stop // 16]
+                    nc.vector.tensor_tensor(gated[:, h], d_rows[t][:].indirect(picks), y_row[:, h], ALU.mult)
+            for h in halves if t == last else [slice(0, S)]:
                 picks = lists["n1"][:, h.start // 16 : h.stop // 16]
                 nc.vector.tensor_tensor(neg_z[:, t, h], win_b[t][:].indirect(picks), gated[:, h], ALU.subtract)
-        nc.scalar.activation(warm_out[:, 1:2], gate[:, S - 1 : S], ACT.Exp)
+        nc.scalar.activation(warm_out[:, 1:2], d_rows[last][:, 0:1], ACT.Exp)
 
         z_bf = sb("z_bf", [P, PACK * S], BF16)
         z_codes = sb("z_codes", [P, S], U32)
@@ -167,30 +185,33 @@ def tile_picked_twcgateblse_none_p_kernel(
             nc.vector.quantize_mx(
                 out=z_codes[:, h].bitcast(FP8X4), scales=z_scales[:, h], in_=z_bf[:, PACK * h.start : PACK * h.stop]
             )
-        s_acc = [product("bank_a", t, (dealt_words, dealt_bytes), (z_codes, z_scales)) for t in range(PACK)]
+        dealt = (dealt_words, dealt_bytes)
+        s0_halves = [product("bank_" + "ab"[i], 0, dealt, (z_codes, z_scales), h) for i, h in enumerate(halves)]
+        s_acc = [None] + [product("bank_a", t, dealt, (z_codes, z_scales)) for t in range(1, PACK)]
 
-        def exp_of_scores(dst, t):
-            nc.scalar.activation(dst, s_acc[t][:], ACT.Exp, scale=0.0625)
+        def from_scores(dst, t, func, scale):
+            if t == 0:
+                for acc, h in zip(s0_halves, halves):
+                    nc.scalar.activation(dst[:, h], acc[:], func, scale=scale)
+            else:
+                nc.scalar.activation(dst[:, :S], s_acc[t][:], func, scale=scale)
 
         sums = []
         for t in range(PACK):
             ex = sb("ex%d" % t, [P, S], F32)
-            exp_of_scores(win_b[t][:, :S], t)
-            if t < 2:
-                exp_of_scores(ex[:], t)
+            from_scores(win_b[t], t, ACT.Exp, 0.0625)
+            if t in (1, 2):
+                from_scores(ex, t, ACT.Exp, 0.0625)
             else:
                 nc.vector.tensor_copy(ex[:], win_b[t][:, :S])
-            if t == 0:
-                nc.vector.tensor_scalar(win_a[1][:, :S], s_acc[1][:], -0.0625, None, ALU.mult)
             total = sb("sum%d" % t, [P, S], F32)
             nc.vector.tensor_tensor(total[:], win_b[t][:].indirect(lists["n3"][:]), ex[:], ALU.add)
             sums.append(total)
         out_rows = out.rearrange("(p t) j -> p t j", t=PACK)
-        for t in (1, 0, 2, 3):
+        for t in range(PACK):
             logs = sb("logs%d" % t, [P, S], F32)
             nc.scalar.activation(logs[:], sums[t][:], ACT.Ln)
-            if t != 1:
-                nc.scalar.activation(win_a[t][:, :S], s_acc[t][:], ACT.Copy, scale=-0.0625)
+            from_scores(win_a[t], t, ACT.Copy, -0.0625)
             result = sb("result%d" % t, [P, S], F32)
             for h in halves if t == PACK - 1 else [slice(0, S)]:
                 picks = lists["n4"][:, h.start // 16 : h.stop // 16]

@@ -58,19 +58,16 @@ def tile_picked_twcgateblse_none_p_kernel(
         load_list("n3", n3)
         load_list("n4", n4)
 
+        warm = sb("warm", [P, 2], F32)
+        nc.vector.memset(warm[:], 0.0)
         table_bytes = sb("table_bytes", [P, T], U8)
         nc.vector.memset(table_bytes[:].bitcast(I32), 0)
-        warm = sb("warm", [P, 2], F32)
-        nc.gpsimd.memset(warm[:], 0.0)
         warm_out = sb("warm_out", [P, 2], F32)
         nc.scalar.activation(warm_out[:, 0:1], warm[:, 0:1], ACT.Sigmoid)
 
         win_b = [sb("win_b%d" % t, [P, WINDOW], F32) for t in range(PACK)]
-        spare = [sb("spare%d" % t, [P, WINDOW], F32) for t in range(2)]
-        for t in range(2):
+        for t in range(PACK):
             nc.vector.memset(win_b[t][:, S:], 0.0)
-            nc.gpsimd.memset(win_b[t + 2][:, S:], 0.0)
-            nc.gpsimd.memset(spare[t][:, S:], 0.0)
         for q in range(4):
             rows = slice(32 * q, 32 * q + 4)
             nc.vector.tensor_copy(table_bytes[rows, :].bitcast(I32), scale_rows[rows, :])
@@ -139,7 +136,8 @@ def tile_picked_twcgateblse_none_p_kernel(
 
         halves = [slice(0, S // 2), slice(S // 2, S)]
         neg_z = sb("neg_z", [P, PACK, S], F32)
-        win_a = [raw[:].rearrange("p j c -> p (j c)") for raw in (w2_raw, neg_z)] + [spare[0][:], spare[1][:]]
+        gated_pairs = [sb("gated_pair%d" % u, [P, WINDOW], F32) for u in range(2)]
+        win_a = [raw[:].rearrange("p j c -> p (j c)") for raw in (w2_raw, neg_z)] + [pair[:] for pair in gated_pairs]
         last = PACK - 1
         d_slots = ["w1_raw0", "w1_bf", "gate0", "gate1"]
         d_rows = []
@@ -150,7 +148,7 @@ def tile_picked_twcgateblse_none_p_kernel(
 
         empty_d(0)
         for t in range(PACK):
-            gated = sb("gated%d" % t, [P, S], F32)
+            gated = gated_pairs[t // 2][:, S * (t % 2) : S * (t % 2 + 1)]
             if t < last:
                 gate = sb("gate%d" % t, [P, S], F32)
                 for h in halves:
@@ -159,7 +157,7 @@ def tile_picked_twcgateblse_none_p_kernel(
                 if t + 1 < last:
                     empty_d(t + 1)
                 nc.scalar.activation(win_b[t][:, :S], y_acc[t][:], ACT.Copy, scale=half_gain[:, t : t + 1])
-                nc.vector.scalar_tensor_tensor(gated[:], y_acc[t][:], gain[:, t : t + 1], gate[:], ALU.mult, ALU.mult)
+                nc.vector.scalar_tensor_tensor(gated, y_acc[t][:], gain[:, t : t + 1], gate[:], ALU.mult, ALU.mult)
             else:
                 empty_d(t)
                 y_row = sb("y_row", [P, S], F32, "gate0")

@@ -17,7 +17,14 @@ ALU = mybir.AluOpType
 
 P = 128
 PACK = 4
+QUADRANT = 32
+STRIPE = 16
+LINE = 16
+SCORE_SCALE = 0.0625
 WINDOW = 2 * S
+WHOLE = slice(0, S)
+HALVES = [slice(0, S // 2), slice(S // 2, S)]
+LAST = PACK - 1
 
 
 def tile_picked_twcgateblse_none_p_kernel(
@@ -28,27 +35,31 @@ def tile_picked_twcgateblse_none_p_kernel(
         keep = ctx.enter_context(tc.tile_pool(name="keep", bufs=1))
         psum = ctx.enter_context(tc.psum_pool(name="psum", bufs=1))
 
-        def sb(name, shape, dtype, tag=None):
-            return keep.tile(shape, dtype, name=name, tag=tag or name, align_bytes=64)
+        def sb(name, shape, dtype, slot=None):
+            return keep.tile(shape, dtype, name=name, tag=slot or name, align_bytes=64)
 
         lists = {}
 
         def load_list(name, src):
-            lists[name] = keep.tile([P, S // 16], U16, name="list_" + name)
+            lists[name] = keep.tile([P, S // STRIPE], U16, name="list_" + name)
             nc.sync.dma_start(lists[name][:], src)
 
+        def picks(name, places):
+            return lists[name][:, places.start // STRIPE : places.stop // STRIPE]
+
+        quadrants = [slice(QUADRANT * q, QUADRANT * q + PACK) for q in range(P // QUADRANT)]
         scale_rows = sb("scale_rows", [P, T // 4], I32)
-        for q in range(4):
-            nc.sync.dma_start(scale_rows[32 * q : 32 * q + 4, :], x_scales[0, 4 * q : 4 * q + 4, :].bitcast(I32))
+        for q, rows in enumerate(quadrants):
+            nc.sync.dma_start(scale_rows[rows, :], x_scales[0, PACK * q : PACK * (q + 1), :].bitcast(I32))
         load_list("two", two)
         w2_raw = sb("w2_raw", [P, PACK, H], F32)
         nc.sync.dma_start(w2_raw[:], w2.rearrange("(p j) c -> p j c", j=PACK))
         load_list("offs", offs)
         load_list("cand", cand)
-        w1_rows = w1.rearrange("(p j) c -> p j c", j=PACK)
-        w1_raw = [sb("w1_raw%d" % h, [P, PACK, H // 2], F32) for h in range(2)]
         table_words = sb("table_words", [P, T], I32)
         nc.sync.dma_start(table_words[:], x_words[0].rearrange("p n t -> p (n t)").bitcast(I32))
+        w1_rows = w1.rearrange("(p j) c -> p j c", j=PACK)
+        w1_raw = [sb("w1_raw%d" % u, [P, PACK, H // 2], F32) for u in range(2)]
         nc.sync.dma_start(w1_raw[0][:], w1_rows[:, :, : H // 2])
         nc.sync.dma_start(w1_raw[1][:], w1_rows[:, :, H // 2 :])
         gain = sb("gain", [P, PACK], F32)
@@ -58,42 +69,50 @@ def tile_picked_twcgateblse_none_p_kernel(
         load_list("n3", n3)
         load_list("n4", n4)
 
-        warm = sb("warm", [P, 2], F32)
-        nc.vector.memset(warm[:], 0.0)
+        zero = sb("zero", [P, 1], F32)
+        nc.vector.memset(zero[:], 0.0)
         table_bytes = sb("table_bytes", [P, T], U8)
         nc.vector.memset(table_bytes[:].bitcast(I32), 0)
-        warm_out = sb("warm_out", [P, 2], F32)
-        nc.scalar.activation(warm_out[:, 0:1], warm[:, 0:1], ACT.Sigmoid)
+        filler = sb("filler", [P, 1], F32)
+        nc.scalar.activation(filler[:], zero[:], ACT.Sigmoid)
 
-        win_b = [sb("win_b%d" % t, [P, WINDOW], F32) for t in range(PACK)]
-        for t in range(PACK):
-            nc.vector.memset(win_b[t][:, S:], 0.0)
-        for q in range(4):
-            rows = slice(32 * q, 32 * q + 4)
+        row_windows = [sb("row_window%d" % t, [P, WINDOW], F32) for t in range(PACK)]
+        for window in row_windows:
+            nc.scalar.copy(window[:, S:], filler[:].to_broadcast([P, WINDOW - S]))
+
+        for rows in quadrants:
             nc.vector.tensor_copy(table_bytes[rows, :].bitcast(I32), scale_rows[rows, :])
 
-        def gather_bytes(name, tag=None):
-            picked = sb("bytes_" + name, [P, S], U8, tag)
+        def gather_bytes(name):
+            picked = sb("bytes_" + name, [P, S], U8)
             nc.vector.tensor_copy(picked[:], table_bytes[:].indirect(lists[name][:]))
             return picked
 
-        def gather_words(name, tag=None):
-            picked = sb("words_" + name, [P, S], U32, tag)
+        def gather_words(name, slot=None):
+            picked = sb("words_" + name, [P, S], U32, slot)
             nc.vector.tensor_copy(picked[:], table_words[:].bitcast(U32).indirect(lists[name][:]))
             return picked
+
+        def deal(name, picked, dtype, run, slot=None):
+            dealt = sb(name, [P, C], dtype, slot)
+            nc.vector.tensor_copy(
+                dealt[:].rearrange("p (t a b) -> p a t b", t=PACK, b=run),
+                picked[:].rearrange("p (a b t) -> p a t b", t=PACK, b=run),
+            )
+            return dealt
 
         def cast_weight(copy, grouped, raw, m0, m1):
             dst = grouped[:].rearrange("p (t m j) -> p m t j", t=PACK, j=PACK)
             copy(dst[:, m0:m1], raw[:].rearrange("p j (m t) -> p m t j", t=PACK))
 
-        def quantize(name, grouped):
+        def quantize_weight(name, grouped):
             codes = sb(name + "_codes", [P, H], U32)
             scales = sb(name + "_scales", [P, H], U8)
             nc.vector.quantize_mx(out=codes[:].bitcast(FP8X4), scales=scales[:], in_=grouped[:])
             return codes, scales
 
-        def product(tag, t, lhs, rhs, places=slice(0, S)):
-            acc = psum.tile([P, places.stop - places.start], F32, name=tag + str(t), tag=tag + str(t))
+        def product(banks, t, lhs, rhs, places=WHOLE):
+            acc = psum.tile([P, places.stop - places.start], F32, name=banks + str(t), tag=banks + str(t))
             cols = slice(P * t, P * (t + 1))
             nc.tensor.matmul_mx(
                 out=acc[:],
@@ -113,105 +132,98 @@ def tile_picked_twcgateblse_none_p_kernel(
         cast_weight(nc.scalar.copy, w2_bf, w2_raw, 0, P)
         w1_bf = sb("w1_bf", [P, PACK * H], BF16)
         cast_weight(nc.scalar.copy, w1_bf, w1_raw[0], 0, P // 2)
-        w2_q = quantize("w2", w2_bf)
+        w2_mx = quantize_weight("w2", w2_bf)
         two_words = gather_words("two")
-        d_acc = [product("bank_a", t, w2_q, (two_words, two_bytes)) for t in range(PACK)]
-        dealt_bytes = sb("dealt_bytes", [P, C], U8, "w2_bf")
-        nc.vector.tensor_copy(
-            dealt_bytes[:].rearrange("p (t a b) -> p a t b", t=PACK, b=16),
-            cand_bytes[:].rearrange("p (a b t) -> p a t b", t=PACK, b=16),
-        )
+        d_acc = [product("bank_a", t, w2_mx, (two_words, two_bytes)) for t in range(PACK)]
+        dealt_bytes = deal("dealt_bytes", cand_bytes, U8, LINE, "w2_bf")
         cast_weight(nc.vector.tensor_copy, w1_bf, w1_raw[1], P // 2, P)
         offs_words = gather_words("offs")
-        w1_q = quantize("w1", w1_bf)
+        w1_mx = quantize_weight("w1", w1_bf)
         cand_words = gather_words("cand", "w1_raw1")
-        dealt_words = sb("dealt_words", [P, C], U32)
-        nc.vector.tensor_copy(
-            dealt_words[:].rearrange("p (t a b) -> p a t b", t=PACK, b=4),
-            cand_words[:].rearrange("p (a b t) -> p a t b", t=PACK, b=4),
-        )
-        y_acc = [product("bank_b", t, w1_q, (offs_words, offs_bytes)) for t in range(PACK)]
+        dealt_words = deal("dealt_words", cand_words, U32, LINE // 4)
+        y_acc = [product("bank_b", t, w1_mx, (offs_words, offs_bytes)) for t in range(PACK)]
         half_gain = sb("half_gain", [P, PACK], F32)
-        nc.gpsimd.tensor_scalar(half_gain[:], gain[:], 0.5, 0.0, ALU.mult, ALU.add)
+        nc.scalar.activation(half_gain[:], gain[:], ACT.Copy, scale=0.5)
 
-        halves = [slice(0, S // 2), slice(S // 2, S)]
         neg_z = sb("neg_z", [P, PACK, S], F32)
-        gated_pairs = [sb("gated_pair%d" % u, [P, WINDOW], F32) for u in range(2)]
-        win_a = [raw[:].rearrange("p j c -> p (j c)") for raw in (w2_raw, neg_z)] + [pair[:] for pair in gated_pairs]
-        last = PACK - 1
+        gated_pairs = [sb("gated_pair%d" % u, [P, WINDOW], F32) for u in range(PACK // 2)]
         d_slots = ["w1_raw0", "w1_bf", "gate0", "gate1"]
         d_rows = []
 
-        def empty_d(t):
+        def empty_d(t, func):
             d_rows.append(sb("d_row%d" % t, [P, S], F32, d_slots[t]))
-            nc.scalar.activation(d_rows[t][:], d_acc[t][:], ACT.Sigmoid if t == last else ACT.Copy)
+            nc.scalar.activation(d_rows[t][:], d_acc[t][:], func)
 
-        empty_d(0)
+        def empty_y(dst, t, factor):
+            nc.scalar.activation(dst, y_acc[t][:], ACT.Copy, scale=factor[:, t : t + 1])
+
+        empty_d(0, ACT.Copy)
         for t in range(PACK):
             gated = gated_pairs[t // 2][:, S * (t % 2) : S * (t % 2 + 1)]
-            if t < last:
+            if t < LAST:
                 gate = sb("gate%d" % t, [P, S], F32)
-                for h in halves:
-                    picks = lists["n2"][:, h.start // 16 : h.stop // 16]
-                    nc.scalar.activation(gate[:, h], d_rows[t][:].indirect(picks), ACT.Sigmoid)
-                if t + 1 < last:
-                    empty_d(t + 1)
-                nc.scalar.activation(win_b[t][:, :S], y_acc[t][:], ACT.Copy, scale=half_gain[:, t : t + 1])
+                for h in HALVES:
+                    nc.scalar.activation(gate[:, h], d_rows[t][:].indirect(picks("n2", h)), ACT.Sigmoid)
+                if t + 1 < LAST:
+                    empty_d(t + 1, ACT.Copy)
+                empty_y(row_windows[t][:, WHOLE], t, half_gain)
                 nc.vector.scalar_tensor_tensor(gated, y_acc[t][:], gain[:, t : t + 1], gate[:], ALU.mult, ALU.mult)
             else:
-                empty_d(t)
+                empty_d(t, ACT.Sigmoid)
                 y_row = sb("y_row", [P, S], F32, "gate0")
-                nc.scalar.activation(y_row[:], y_acc[t][:], ACT.Copy, scale=gain[:, t : t + 1])
-                nc.scalar.activation(win_b[t][:, :S], y_acc[t][:], ACT.Copy, scale=half_gain[:, t : t + 1])
-                for h in halves:
-                    picks = lists["n2"][:, h.start // 16 : h.stop // 16]
-                    nc.vector.tensor_tensor(gated[:, h], d_rows[t][:].indirect(picks), y_row[:, h], ALU.mult)
-            for h in halves if t == last else [slice(0, S)]:
-                picks = lists["n1"][:, h.start // 16 : h.stop // 16]
-                nc.vector.tensor_tensor(neg_z[:, t, h], win_b[t][:].indirect(picks), gated[:, h], ALU.subtract)
-        nc.scalar.activation(warm_out[:, 1:2], d_rows[last][:, 0:1], ACT.Exp)
+                empty_y(y_row[:], t, gain)
+                empty_y(row_windows[t][:, WHOLE], t, half_gain)
+                for h in HALVES:
+                    nc.vector.tensor_tensor(gated[:, h], d_rows[t][:].indirect(picks("n2", h)), y_row[:, h], ALU.mult)
+            for h in HALVES if t == LAST else [WHOLE]:
+                nc.vector.tensor_tensor(
+                    neg_z[:, t, h], row_windows[t][:].indirect(picks("n1", h)), gated[:, h], ALU.subtract
+                )
+        exp_warm = sb("exp_warm", [P, 1], F32)
+        nc.scalar.activation(exp_warm[:], d_rows[LAST][:, 0:1], ACT.Exp)
 
         z_bf = sb("z_bf", [P, PACK * S], BF16)
         z_codes = sb("z_codes", [P, S], U32)
         z_scales = sb("z_scales", [P, S], U8)
         z_dst = z_bf[:].rearrange("p (c i t) -> p c t i", t=PACK, i=4)
         z_src = neg_z[:].rearrange("p t (c i) -> p c t i", i=4)
-        mid = S // 8
+        mid = S // 2 // 4
         nc.scalar.activation(z_dst[:, :mid], z_src[:, :mid], ACT.Copy, scale=-1.0)
         nc.vector.tensor_scalar(z_dst[:, mid:], z_src[:, mid:], -1.0, None, ALU.mult)
-        for h in halves:
+        for h in HALVES:
             nc.vector.quantize_mx(
                 out=z_codes[:, h].bitcast(FP8X4), scales=z_scales[:, h], in_=z_bf[:, PACK * h.start : PACK * h.stop]
             )
-        dealt = (dealt_words, dealt_bytes)
-        s0_halves = [product("bank_" + "ab"[i], 0, dealt, (z_codes, z_scales), h) for i, h in enumerate(halves)]
-        s_acc = [None] + [product("bank_a", t, dealt, (z_codes, z_scales)) for t in range(1, PACK)]
+
+        cand_mx = (dealt_words, dealt_bytes)
+        z_mx = (z_codes, z_scales)
+        s_acc = [[(product(banks, 0, cand_mx, z_mx, h), h) for banks, h in zip(("bank_a", "bank_b"), HALVES)]]
+        s_acc.extend([(product("bank_a", t, cand_mx, z_mx), WHOLE)] for t in range(1, PACK))
 
         def from_scores(dst, t, func, scale):
-            if t == 0:
-                for acc, h in zip(s0_halves, halves):
-                    nc.scalar.activation(dst[:, h], acc[:], func, scale=scale)
-            else:
-                nc.scalar.activation(dst[:, :S], s_acc[t][:], func, scale=scale)
+            for acc, places in s_acc[t]:
+                nc.scalar.activation(dst[:, places], acc[:], func, scale=scale)
 
         sums = []
         for t in range(PACK):
             ex = sb("ex%d" % t, [P, S], F32)
-            from_scores(win_b[t], t, ACT.Exp, 0.0625)
-            if t in (1, 2):
-                from_scores(ex, t, ACT.Exp, 0.0625)
+            from_scores(row_windows[t], t, ACT.Exp, SCORE_SCALE)
+            if 0 < t < LAST:
+                from_scores(ex, t, ACT.Exp, SCORE_SCALE)
             else:
-                nc.vector.tensor_copy(ex[:], win_b[t][:, :S])
+                nc.vector.tensor_copy(ex[:], row_windows[t][:, WHOLE])
             total = sb("sum%d" % t, [P, S], F32)
-            nc.vector.tensor_tensor(total[:], win_b[t][:].indirect(lists["n3"][:]), ex[:], ALU.add)
+            nc.vector.tensor_tensor(total[:], row_windows[t][:].indirect(lists["n3"][:]), ex[:], ALU.add)
             sums.append(total)
+
+        neg_s_windows = [wide[:].rearrange("p j c -> p (j c)") for wide in (w2_raw, neg_z)]
+        neg_s_windows.extend(pair[:] for pair in gated_pairs)
         out_rows = out.rearrange("(p t) j -> p t j", t=PACK)
         for t in range(PACK):
             logs = sb("logs%d" % t, [P, S], F32)
             nc.scalar.activation(logs[:], sums[t][:], ACT.Ln)
-            from_scores(win_a[t], t, ACT.Copy, -0.0625)
+            from_scores(neg_s_windows[t], t, ACT.Copy, -SCORE_SCALE)
             result = sb("result%d" % t, [P, S], F32)
-            for h in halves if t == PACK - 1 else [slice(0, S)]:
-                picks = lists["n4"][:, h.start // 16 : h.stop // 16]
-                nc.vector.tensor_tensor(result[:, h], win_a[t].indirect(picks), logs[:, h], ALU.add)
+            for h in HALVES if t == LAST else [WHOLE]:
+                nc.vector.tensor_tensor(result[:, h], neg_s_windows[t].indirect(picks("n4", h)), logs[:, h], ALU.add)
                 nc.sync.dma_start(out_rows[:, t, h], result[:, h])

from contextlib import ExitStack

import concourse.mybir as mybir

K, T, S, H, C = 512, 2048, 512, 512, 512
FLOPS = 2 * K * S * (H + H + C)

F32 = mybir.dt.float32
BF16 = mybir.dt.bfloat16
I32 = mybir.dt.int32
U32 = mybir.dt.uint32
U16 = mybir.dt.uint16
U8 = mybir.dt.uint8
FP8X4 = mybir.dt.float8_e4m3fn_x4
ACT = mybir.ActivationFunctionType
ALU = mybir.AluOpType

P = 128
PACK = 4
QUADRANT = 32
STRIPE = 16
LINE = 16
SCORE_SCALE = 0.0625
WINDOW = 2 * S
WHOLE = slice(0, S)
HALVES = [slice(0, S // 2), slice(S // 2, S)]
LAST = PACK - 1


def tile_picked_twcgateblse_none_p_kernel(
    tc, x_words, x_scales, w1, w2, gs, offs, two, n1, n2, cand, n3, n4, out
):
    nc = tc.nc
    with ExitStack() as ctx:
        keep = ctx.enter_context(tc.tile_pool(name="keep", bufs=1))
        psum = ctx.enter_context(tc.psum_pool(name="psum", bufs=1))

        def sb(name, shape, dtype, slot=None):
            return keep.tile(shape, dtype, name=name, tag=slot or name, align_bytes=64)

        lists = {}

        def load_list(name, src):
            lists[name] = keep.tile([P, S // STRIPE], U16, name="list_" + name)
            nc.sync.dma_start(lists[name][:], src)

        def picks(name, places):
            return lists[name][:, places.start // STRIPE : places.stop // STRIPE]

        quadrants = [slice(QUADRANT * q, QUADRANT * q + PACK) for q in range(P // QUADRANT)]
        scale_rows = sb("scale_rows", [P, T // 4], I32)
        for q, rows in enumerate(quadrants):
            nc.sync.dma_start(scale_rows[rows, :], x_scales[0, PACK * q : PACK * (q + 1), :].bitcast(I32))
        load_list("two", two)
        w2_raw = sb("w2_raw", [P, PACK, H], F32)
        nc.sync.dma_start(w2_raw[:], w2.rearrange("(p j) c -> p j c", j=PACK))
        load_list("offs", offs)
        load_list("cand", cand)
        table_words = sb("table_words", [P, T], I32)
        nc.sync.dma_start(table_words[:], x_words[0].rearrange("p n t -> p (n t)").bitcast(I32))
        w1_rows = w1.rearrange("(p j) c -> p j c", j=PACK)
        w1_raw = [sb("w1_raw%d" % u, [P, PACK, H // 2], F32) for u in range(2)]
        nc.sync.dma_start(w1_raw[0][:], w1_rows[:, :, : H // 2])
        nc.sync.dma_start(w1_raw[1][:], w1_rows[:, :, H // 2 :])
        gain = sb("gain", [P, PACK], F32)
        nc.sync.dma_start(gain[:], gs.rearrange("(p t) o -> p (t o)", t=PACK))
        load_list("n2", n2)
        load_list("n1", n1)
        load_list("n3", n3)
        load_list("n4", n4)

        zero = sb("zero", [P, 1], F32)
        nc.vector.memset(zero[:], 0.0)
        table_bytes = sb("table_bytes", [P, T], U8)
        nc.vector.memset(table_bytes[:].bitcast(I32), 0)
        filler = sb("filler", [P, 1], F32)
        nc.scalar.activation(filler[:], zero[:], ACT.Sigmoid)

        row_windows = [sb("row_window%d" % t, [P, WINDOW], F32) for t in range(PACK)]
        for window in row_windows:
            nc.scalar.copy(window[:, S:], filler[:].to_broadcast([P, WINDOW - S]))

        for rows in quadrants:
            nc.vector.tensor_copy(table_bytes[rows, :].bitcast(I32), scale_rows[rows, :])

        def gather_bytes(name):
            picked = sb("bytes_" + name, [P, S], U8)
            nc.vector.tensor_copy(picked[:], table_bytes[:].indirect(lists[name][:]))
            return picked

        def gather_words(name, slot=None):
            picked = sb("words_" + name, [P, S], U32, slot)
            nc.vector.tensor_copy(picked[:], table_words[:].bitcast(U32).indirect(lists[name][:]))
            return picked

        def deal(name, picked, dtype, run, slot=None):
            dealt = sb(name, [P, C], dtype, slot)
            nc.vector.tensor_copy(
                dealt[:].rearrange("p (t a b) -> p a t b", t=PACK, b=run),
                picked[:].rearrange("p (a b t) -> p a t b", t=PACK, b=run),
            )
            return dealt

        def cast_weight(copy, grouped, raw, m0, m1):
            dst = grouped[:].rearrange("p (t m j) -> p m t j", t=PACK, j=PACK)
            copy(dst[:, m0:m1], raw[:].rearrange("p j (m t) -> p m t j", t=PACK))

        def quantize_weight(name, grouped):
            codes = sb(name + "_codes", [P, H], U32)
            scales = sb(name + "_scales", [P, H], U8)
            nc.vector.quantize_mx(out=codes[:].bitcast(FP8X4), scales=scales[:], in_=grouped[:])
            return codes, scales

        def product(banks, t, lhs, rhs, places=WHOLE):
            acc = psum.tile([P, places.stop - places.start], F32, name=banks + str(t), tag=banks + str(t))
            cols = slice(P * t, P * (t + 1))
            nc.tensor.matmul_mx(
                out=acc[:],
                lhsT=lhs[0][:, cols].bitcast(FP8X4),
                lhsT_scale=lhs[1][:, cols],
                rhs=rhs[0][:, places].bitcast(FP8X4),
                rhs_scale=rhs[1][:, places],
                start=True,
                stop=True,
            )
            return acc

        two_bytes = gather_bytes("two")
        offs_bytes = gather_bytes("offs")
        cand_bytes = gather_bytes("cand")
        w2_bf = sb("w2_bf", [P, PACK * H], BF16)
        cast_weight(nc.scalar.copy, w2_bf, w2_raw, 0, P)
        w1_bf = sb("w1_bf", [P, PACK * H], BF16)
        cast_weight(nc.scalar.copy, w1_bf, w1_raw[0], 0, P // 2)
        w2_mx = quantize_weight("w2", w2_bf)
        two_words = gather_words("two")
        d_acc = [product("bank_a", t, w2_mx, (two_words, two_bytes)) for t in range(PACK)]
        dealt_bytes = deal("dealt_bytes", cand_bytes, U8, LINE, "w2_bf")
        cast_weight(nc.vector.tensor_copy, w1_bf, w1_raw[1], P // 2, P)
        offs_words = gather_words("offs")
        w1_mx = quantize_weight("w1", w1_bf)
        cand_words = gather_words("cand", "w1_raw1")
        dealt_words = deal("dealt_words", cand_words, U32, LINE // 4)
        y_acc = [product("bank_b", t, w1_mx, (offs_words, offs_bytes)) for t in range(PACK)]
        half_gain = sb("half_gain", [P, PACK], F32)
        nc.scalar.activation(half_gain[:], gain[:], ACT.Copy, scale=0.5)

        neg_z = sb("neg_z", [P, PACK, S], F32)
        gated_pairs = [sb("gated_pair%d" % u, [P, WINDOW], F32) for u in range(PACK // 2)]
        d_slots = ["w1_raw0", "w1_bf", "gate0", "gate1"]
        d_rows = []

        def empty_d(t, func):
            d_rows.append(sb("d_row%d" % t, [P, S], F32, d_slots[t]))
            nc.scalar.activation(d_rows[t][:], d_acc[t][:], func)

        def empty_y(dst, t, factor):
            nc.scalar.activation(dst, y_acc[t][:], ACT.Copy, scale=factor[:, t : t + 1])

        empty_d(0, ACT.Copy)
        for t in range(PACK):
            gated = gated_pairs[t // 2][:, S * (t % 2) : S * (t % 2 + 1)]
            if t < LAST:
                gate = sb("gate%d" % t, [P, S], F32)
                for h in HALVES:
                    nc.scalar.activation(gate[:, h], d_rows[t][:].indirect(picks("n2", h)), ACT.Sigmoid)
                if t + 1 < LAST:
                    empty_d(t + 1, ACT.Copy)
                empty_y(row_windows[t][:, WHOLE], t, half_gain)
                nc.vector.scalar_tensor_tensor(gated, y_acc[t][:], gain[:, t : t + 1], gate[:], ALU.mult, ALU.mult)
            else:
                empty_d(t, ACT.Sigmoid)
                y_row = sb("y_row", [P, S], F32, "gate0")
                empty_y(y_row[:], t, gain)
                empty_y(row_windows[t][:, WHOLE], t, half_gain)
                for h in HALVES:
                    nc.vector.tensor_tensor(gated[:, h], d_rows[t][:].indirect(picks("n2", h)), y_row[:, h], ALU.mult)
            for h in HALVES if t == LAST else [WHOLE]:
                nc.vector.tensor_tensor(
                    neg_z[:, t, h], row_windows[t][:].indirect(picks("n1", h)), gated[:, h], ALU.subtract
                )
        exp_warm = sb("exp_warm", [P, 1], F32)
        nc.scalar.activation(exp_warm[:], d_rows[LAST][:, 0:1], ACT.Exp)

        z_bf = sb("z_bf", [P, PACK * S], BF16)
        z_codes = sb("z_codes", [P, S], U32)
        z_scales = sb("z_scales", [P, S], U8)
        z_dst = z_bf[:].rearrange("p (c i t) -> p c t i", t=PACK, i=4)
        z_src = neg_z[:].rearrange("p t (c i) -> p c t i", i=4)
        mid = S // 2 // 4
        nc.scalar.activation(z_dst[:, :mid], z_src[:, :mid], ACT.Copy, scale=-1.0)
        nc.vector.tensor_scalar(z_dst[:, mid:], z_src[:, mid:], -1.0, None, ALU.mult)
        for h in HALVES:
            nc.vector.quantize_mx(
                out=z_codes[:, h].bitcast(FP8X4), scales=z_scales[:, h], in_=z_bf[:, PACK * h.start : PACK * h.stop]
            )

        cand_mx = (dealt_words, dealt_bytes)
        z_mx = (z_codes, z_scales)
        s_acc = [[(product(banks, 0, cand_mx, z_mx, h), h) for banks, h in zip(("bank_a", "bank_b"), HALVES)]]
        s_acc.extend([(product("bank_a", t, cand_mx, z_mx), WHOLE)] for t in range(1, PACK))

        def from_scores(dst, t, func, scale):
            for acc, places in s_acc[t]:
                nc.scalar.activation(dst[:, places], acc[:], func, scale=scale)

        sums = []
        for t in range(PACK):
            ex = sb("ex%d" % t, [P, S], F32)
            from_scores(row_windows[t], t, ACT.Exp, SCORE_SCALE)
            if 0 < t < LAST:
                from_scores(ex, t, ACT.Exp, SCORE_SCALE)
            else:
                nc.vector.tensor_copy(ex[:], row_windows[t][:, WHOLE])
            total = sb("sum%d" % t, [P, S], F32)
            nc.vector.tensor_tensor(total[:], row_windows[t][:].indirect(lists["n3"][:]), ex[:], ALU.add)
            sums.append(total)

        neg_s_windows = [wide[:].rearrange("p j c -> p (j c)") for wide in (w2_raw, neg_z)]
        neg_s_windows.extend(pair[:] for pair in gated_pairs)
        out_rows = out.rearrange("(p t) j -> p t j", t=PACK)
        for t in range(PACK):
            logs = sb("logs%d" % t, [P, S], F32)
            nc.scalar.activation(logs[:], sums[t][:], ACT.Ln)
            from_scores(neg_s_windows[t], t, ACT.Copy, -SCORE_SCALE)
            result = sb("result%d" % t, [P, S], F32)
            for h in HALVES if t == LAST else [WHOLE]:
                nc.vector.tensor_tensor(result[:, h], neg_s_windows[t].indirect(picks("n4", h)), logs[:, h], ALU.add)
                nc.sync.dma_start(out_rows[:, t, h], result[:, h])
